import numpy as np
import ml_dtypes


def mxq(x, axis, fmt="e4m3"):
    dtype, down = {"e4m3": (ml_dtypes.float8_e4m3fn, 7), "e5m2": (ml_dtypes.float8_e5m2, 14)}[fmt]
    v = np.moveaxis(np.asarray(x, np.float32).astype(ml_dtypes.bfloat16).astype(np.float64), axis, -1)
    blocks = v.reshape(v.shape[:-1] + (-1, 32))
    amax = np.abs(blocks).max(-1, keepdims=True)
    byte = np.maximum(np.where(amax > 0, np.frexp(amax)[1] - 1 + 127, 0) - down, 1)
    scale = np.exp2(byte - 127.0)
    codes = (blocks / scale).astype(np.float32).astype(dtype).astype(np.float64)
    return np.moveaxis((codes * scale).reshape(v.shape), -1, axis)


WIDE = False


def mx_kscale(k):
    if not WIDE:
        return np.ones(k)
    levels = np.array([10, -10, 5, -5, 0])
    if k % 512:
        return np.exp2(np.random.permutation(np.resize(levels, k // 32))).repeat(32)
    a = np.empty((k // 512, 16))
    for p in range(k // 512):
        a[p, :8] = np.random.permutation(np.resize(levels, 8))
        for g in range(8):
            far = levels[np.abs(levels - a[p, g]) >= 10]
            a[p, g + 8] = far[np.random.randint(len(far))]
    return np.exp2(a.ravel()).repeat(32)


def f64(x):
    return np.asarray(x).astype(np.float64)


def striped(idx):
    return np.tile(idx.reshape(-1, 16).T, (8, 1)).astype(np.uint16)


def unstriped(offs):
    return offs[:16].T.reshape(-1).astype(np.int64)


E2M1 = np.array([0.0, 0.5, 1.0, 1.5, 2.0, 3.0, 4.0, 6.0, -0.0, -0.5, -1.0, -1.5, -2.0, -3.0, -4.0, -6.0])


def pack_weight(w, fmt):
    k, n = w.shape
    w = f64(np.asarray(w, np.float32).astype(ml_dtypes.bfloat16)).reshape(k // 32, 32, n)
    amax = np.abs(w).max(1)
    if fmt == "e4m3":
        byte = np.frexp(amax)[1] - 1 + 127 - 7
    else:
        mant, ex = np.frexp(amax / 6.0)
        byte = np.where(mant > 0.5, ex, ex - 1) + 127
    byte = np.clip(np.where(amax > 0, byte, 1), 1, 254)
    scaled = (w * np.exp2(127.0 - byte)[:, None, :]).reshape(k, n).astype(np.float32)
    by_word = np.ascontiguousarray(scaled.reshape(k // 512, 128, 4, n).transpose(0, 1, 3, 2))
    if fmt == "e4m3":
        words = by_word.astype(ml_dtypes.float8_e4m3fn).view(np.uint8)
    else:
        c = by_word.astype(ml_dtypes.float4_e2m1fn).view(np.uint8) & 0xF
        words = (c[..., 0::2] | (c[..., 1::2] << 4)).reshape(k // 512, 128, 2 * n)
    return np.ascontiguousarray(words), np.ascontiguousarray(byte.astype(np.uint8).reshape(k // 512, 16, n))


def unpack_weight(words, scales, fmt):
    g, _, n = scales.shape
    words = np.ascontiguousarray(words).reshape(g, 128, n, -1)
    if fmt == "e4m3":
        vals = words.view(ml_dtypes.float8_e4m3fn).astype(np.float64)
    else:
        nib = np.empty((g, 128, n, 4), np.uint8)
        nib[..., 0::2] = words & 0xF
        nib[..., 1::2] = words >> 4
        vals = E2M1[nib]
    vals = vals * np.repeat(np.exp2(scales.astype(np.float64) - 127.0), 8, axis=1)[..., None]
    return vals.transpose(0, 1, 3, 2).reshape(g * 512, n)


K, T, E, C, N = 1024, 768, 4, 256, 128
PAD = 32
K8 = 512


def by_expert(wq, xq):
    return np.concatenate([wq[e].T @ xq[:, e * C:(e + 1) * C] for e in range(E)], axis=1)


def setup_inputs():
    n = np.random.standard_normal
    s = mx_kscale(K)[:, None]
    first = np.random.permutation(np.repeat(np.arange(E), T // E))
    second = (first + 1 + np.random.permutation(np.repeat(np.arange(E - 1), -(-T // (E - 1)))[:T])) % E
    while np.bincount(second, minlength=E).max() != T // E:
        load = np.bincount(second, minlength=E); hi, lo = int(load.argmax()), int(load.argmin())
        t = np.flatnonzero((second == hi) & (first != lo))[0]; second[t] = lo
    slot_token = np.empty(E * C, np.int64); pos = np.empty((2, T), np.int64); fill = np.zeros(E, np.int64)
    place = np.stack([np.random.permutation(C) for _ in range(E)])
    for r, deal in enumerate((first, second)):
        for t in np.random.permutation(T):
            e = deal[t]
            if fill[e] < C: j = e * C + place[e, fill[e]]; fill[e] += 1; slot_token[j] = t; pos[r, t] = j
            else: pos[r, t] = E * C + t % PAD
    g = np.random.uniform(0.2, 0.8, T)
    w = n((E, K, N)) / np.sqrt(K) / s[None]
    w8 = [pack_weight(m[:K8], "e4m3") for m in w]
    w4 = [pack_weight(m[K8:], "e2m1") for m in w]
    return {
        "xT": (n((K, T)) * s).astype(np.float32),
        "w8_words": np.stack([m[0] for m in w8]),
        "w8_scales": np.stack([m[1] for m in w8]),
        "w4_words": np.stack([m[0] for m in w4]),
        "w4_scales": np.stack([m[1] for m in w4]),
        "b": (0.3 * n((N, E))).astype(np.float32),
        "gate": np.stack([np.tile(g, (N, 1)), np.tile(1.0 - g, (N, 1))]).astype(np.float32),
        "offs": striped(slot_token),
        "pos1": striped(pos[0]),
        "pos2": striped(pos[1]),
    }


def reference(xT, w8_words, w8_scales, w4_words, w4_scales, b, gate, offs, pos1, pos2):
    idx = unstriped(offs)
    w = np.stack([np.concatenate([unpack_weight(w8_words[e], w8_scales[e], "e4m3"), unpack_weight(w4_words[e], w4_scales[e], "e2m1")]) for e in range(E)])
    xq = mxq(f64(xT)[:, idx], 0, "e4m3")
    y = by_expert(w, xq)
    y = y + np.repeat(f64(b), C, axis=1)
    y = np.concatenate([y, np.zeros((N, PAD))], axis=1)
    return f64(gate[0]) * y[:, unstriped(pos1)] + f64(gate[1]) * y[:, unstriped(pos2)]

@@ -1,0 +1,166 @@
+from contextlib import ExitStack
+
+import concourse.mybir as mybir
+
+K, T, E, C, N = 1024, 768, 4, 256, 128
+PAD = 32
+P = 128
+PACK = 4
+SLOTS = E * C
+FLOPS = 2 * K * N * SLOTS
+
+F32 = mybir.dt.float32
+BF16 = mybir.dt.bfloat16
+I32 = mybir.dt.int32
+U32 = mybir.dt.uint32
+U16 = mybir.dt.uint16
+U8 = mybir.dt.uint8
+E4M3X4 = mybir.dt.float8_e4m3fn_x4
+E2M1X4 = mybir.dt.float4_e2m1fn_x4
+
+MULT = mybir.AluOpType.mult
+ADD = mybir.AluOpType.add
+IDENTITY = mybir.ActivationFunctionType.Identity
+
+CHUNKS = (
+    (0, 0, 256, 0),
+    (0, 256, 256, 256),
+    (0, 512, 256, 160),
+    (1, 0, 256, 0),
+    (1, 256, 256, 64),
+    (1, 512, 256, 160),
+)
+SCALE_ROW = (4, 0)
+
+
+def tile_moe_cap2_lin_bias_kernel(
+    tc, xT, w8_words, w8_scales, w4_words, w4_scales, b, gate, offs, pos1, pos2, out
+):
+    nc = tc.nc
+    with ExitStack() as ctx:
+        lists = ctx.enter_context(tc.tile_pool(name="lists", bufs=1))
+        keep = ctx.enter_context(tc.tile_pool(name="keep", bufs=1))
+        psum = ctx.enter_context(tc.psum_pool(name="psum", bufs=1))
+
+        offs_sb = lists.tile([P, SLOTS // 16], U16, name="offs_sb")
+        pos1_sb = lists.tile([P, T // 16], U16, name="pos1_sb")
+        pos2_sb = lists.tile([P, T // 16], U16, name="pos2_sb")
+
+        s8 = keep.tile([P, E * N], U8, align_bytes=64, name="s8")
+        s4 = keep.tile([P, E * N], U8, align_bytes=64, name="s4")
+        nc.vector.memset(s8[:].bitcast(I32), 0)
+        nc.vector.memset(s4[:].bitcast(I32), 0)
+        token_bytes = keep.tile([P, T], U8, align_bytes=64, name="token_bytes")
+        nc.gpsimd.memset(token_bytes[:], 0)
+        y = keep.tile([P, SLOTS + PAD], F32, align_bytes=64, name="y")
+        nc.vector.memset(y[:, SLOTS:], 0.0)
+
+        raws = []
+        for i, (a, t0, n, v) in enumerate(CHUNKS):
+            raw = keep.tile([P, PACK, n], F32, align_bytes=64, name="raw%d" % i)
+            rows = xT[a * 512 : (a + 1) * 512, t0 : t0 + n]
+            nc.sync.dma_start(out=raw[:], in_=rows.rearrange("(p j) t -> p j t", j=PACK))
+            raws.append(raw)
+            if i == 1:
+                nc.sync.dma_start(offs_sb[:], offs)
+
+        for plane, scales in ((s8, w8_scales), (s4, w4_scales)):
+            view = plane[:].rearrange("p (e n) -> p e n", e=E)
+            for q in range(4):
+                nc.sync.dma_start(
+                    out=view[32 * q : 32 * q + 4, :, :].bitcast(I32),
+                    in_=scales[:, 0, 4 * q : 4 * q + 4, :].rearrange("e q n -> q e n").bitcast(I32),
+                )
+
+        w8 = keep.tile([P, E, 4 * N], U8, align_bytes=64, name="w8")
+        nc.sync.dma_start(out=w8[:].bitcast(I32), in_=w8_words[:, 0].rearrange("e p n r -> p e (n r)").bitcast(I32))
+        w4 = keep.tile([P, E, 2 * N], U8, align_bytes=64, name="w4")
+        nc.sync.dma_start(out=w4[:].bitcast(I32), in_=w4_words[:, 0].rearrange("e p n -> p e n").bitcast(I32))
+        bias = keep.tile([P, E], F32, name="bias")
+        nc.sync.dma_start(out=bias[:], in_=b)
+        nc.sync.dma_start(pos1_sb[:], pos1)
+        nc.sync.dma_start(pos2_sb[:], pos2)
+        gates = keep.tile([P, 2, T], F32, align_bytes=64, name="gates")
+        nc.sync.dma_start(out=gates[:], in_=gate.rearrange("a p t -> p a t"))
+
+        words = [keep.tile([P, T], U32, align_bytes=64, name="words%d" % a) for a in range(2)]
+        slot_words = [keep.tile([P, SLOTS], U32, align_bytes=64, name="slot_words%d" % a) for a in range(2)]
+        slot_bytes = keep.tile([P, SLOTS], U8, align_bytes=64, name="slot_bytes")
+
+        def cast(i):
+            a, t0, n, v = CHUNKS[i]
+            grouped = keep.tile([P, n, PACK], BF16, align_bytes=64, name="grouped%d" % i)
+            source = raws[i][:].rearrange("p j t -> p t j")
+            if v < n:
+                nc.scalar.copy(grouped[:, v:n, :], source[:, v:n, :])
+            if v > 0:
+                nc.vector.tensor_copy(grouped[:, 0:v, :], source[:, 0:v, :])
+            return grouped
+
+        def quantise(i, grouped):
+            a, t0, n, v = CHUNKS[i]
+            nc.vector.quantize_mx(
+                out=words[a][:, t0 : t0 + n].bitcast(E4M3X4),
+                scales=token_bytes[SCALE_ROW[a] : P, t0 : t0 + n],
+                in_=grouped[:].rearrange("p t j -> p (t j)"),
+            )
+
+        def gather(dst, src, s0, n):
+            nc.vector.tensor_copy(dst[:, s0 : s0 + n], src[:].indirect(offs_sb[:, s0 // 16 : (s0 + n) // 16]))
+
+        g = [cast(0), cast(1)]
+        quantise(0, g[0])
+        g.append(cast(2))
+        quantise(1, g[1])
+        quantise(2, g[2])
+        g.append(cast(3))
+        gather(slot_words[0], words[0], 0, 512)
+        gather(slot_words[0], words[0], 512, 512)
+        g.append(cast(4))
+        quantise(3, g[3])
+        g.append(cast(5))
+        quantise(4, g[4])
+        quantise(5, g[5])
+
+        banks = {}
+
+        def multiply(s0):
+            e = s0 // C
+            bank = psum.tile([P, 128], F32, name="bank%d" % (s0 // 128))
+            nc.tensor.matmul_mx(
+                out=bank[:],
+                lhsT=w8[:, e, :].bitcast(E4M3X4),
+                lhsT_scale=s8[:, e * N : (e + 1) * N],
+                rhs=slot_words[0][:, s0 : s0 + 128].bitcast(E4M3X4),
+                rhs_scale=slot_bytes[SCALE_ROW[0] : P, s0 : s0 + 128],
+                start=True,
+                stop=False,
+            )
+            nc.tensor.matmul_mx(
+                out=bank[:],
+                lhsT=w4[:, e, :].bitcast(E2M1X4),
+                lhsT_scale=s4[:, e * N : (e + 1) * N],
+                rhs=slot_words[1][:, s0 : s0 + 128].bitcast(E4M3X4),
+                rhs_scale=slot_bytes[SCALE_ROW[1] : P, s0 : s0 + 128],
+                start=False,
+                stop=True,
+            )
+            nc.scalar.activation(y[:, s0 : s0 + 128], bank[:], IDENTITY, bias=bias[:, e : e + 1], scale=1.0)
+
+        for s0, n in ((0, 512), (512, 384), (896, 128)):
+            gather(slot_bytes, token_bytes, s0, n)
+            gather(slot_words[1], words[1], s0, n)
+            for s in range(s0, s0 + n, 128):
+                multiply(s)
+
+        first = keep.tile([P, T], F32, align_bytes=64, name="first")
+        second = keep.tile([P, T], F32, align_bytes=64, name="second")
+        result = keep.tile([P, T], F32, align_bytes=64, name="result")
+        PARTS = ((0, 512), (512, 256))
+        for t0, n in PARTS:
+            cols = slice(t0, t0 + n)
+            entries = slice(t0 // 16, (t0 + n) // 16)
+            nc.vector.tensor_tensor(first[:, cols], y[:].indirect(pos1_sb[:, entries]), gates[:, 0, cols], MULT)
+            nc.vector.tensor_tensor(second[:, cols], y[:].indirect(pos2_sb[:, entries]), gates[:, 1, cols], MULT)
+            nc.vector.tensor_tensor(result[:, cols], first[:, cols], second[:, cols], ADD)
+            nc.sync.dma_start(out=out[:, cols], in_=result[:, cols])

@@ -22,14 +22,8 @@ MULT = mybir.AluOpType.mult
 ADD = mybir.AluOpType.add
 IDENTITY = mybir.ActivationFunctionType.Identity
 
-CHUNKS = (
-    (0, 0, 256, 0),
-    (0, 256, 256, 256),
-    (0, 512, 256, 160),
-    (1, 0, 256, 0),
-    (1, 256, 256, 64),
-    (1, 512, 256, 160),
-)
+PAIR_VECTOR = 512
+CHUNKS = ((0, 256, 0), (256, 256, 0), (512, 256, 160))
 SCALE_ROW = (4, 0)
 
 
@@ -55,22 +49,26 @@ def tile_moe_cap2_lin_bias_kernel(
         y = keep.tile([P, SLOTS + PAD], F32, align_bytes=64, name="y")
         nc.vector.memset(y[:, SLOTS:], 0.0)
 
-        raws = []
-        for i, (a, t0, n, v) in enumerate(CHUNKS):
-            raw = keep.tile([P, PACK, n], F32, align_bytes=64, name="raw%d" % i)
-            rows = xT[a * 512 : (a + 1) * 512, t0 : t0 + n]
-            nc.sync.dma_start(out=raw[:], in_=rows.rearrange("(p j) t -> p j t", j=PACK))
-            raws.append(raw)
-            if i == 1:
-                nc.sync.dma_start(offs_sb[:], offs)
-
-        for plane, scales in ((s8, w8_scales), (s4, w4_scales)):
+        for plane, scales, queue in ((s4, w4_scales, nc.scalar), (s8, w8_scales, nc.gpsimd)):
             view = plane[:].rearrange("p (e n) -> p e n", e=E)
             for q in range(4):
-                nc.sync.dma_start(
+                queue.dma_start(
                     out=view[32 * q : 32 * q + 4, :, :].bitcast(I32),
                     in_=scales[:, 0, 4 * q : 4 * q + 4, :].rearrange("e q n -> q e n").bitcast(I32),
                 )
+
+        pairs = []
+        by_row = xT[0:512, :].rearrange("(p j) t -> p j t", j=PACK)
+        for u in range(2):
+            pair = keep.tile([P, 2, T], F32, align_bytes=64, name="pair%d" % u)
+            nc.sync.dma_start(out=pair[:], in_=by_row[:, 2 * u : 2 * u + 2, :])
+            pairs.append(pair)
+        nc.sync.dma_start(offs_sb[:], offs)
+        raws = []
+        for i, (t0, n, v) in enumerate(CHUNKS):
+            raw = keep.tile([P, PACK, n], F32, align_bytes=64, name="raw%d" % i)
+            nc.sync.dma_start(out=raw[:], in_=xT[512:1024, t0 : t0 + n].rearrange("(p j) t -> p j t", j=PACK))
+            raws.append(raw)
 
         w8 = keep.tile([P, E, 4 * N], U8, align_bytes=64, name="w8")
         nc.sync.dma_start(out=w8[:].bitcast(I32), in_=w8_words[:, 0].rearrange("e p n r -> p e (n r)").bitcast(I32))
@@ -87,80 +85,91 @@ def tile_moe_cap2_lin_bias_kernel(
         slot_words = [keep.tile([P, SLOTS], U32, align_bytes=64, name="slot_words%d" % a) for a in range(2)]
         slot_bytes = keep.tile([P, SLOTS], U8, align_bytes=64, name="slot_bytes")
 
-        def cast(i):
-            a, t0, n, v = CHUNKS[i]
-            grouped = keep.tile([P, n, PACK], BF16, align_bytes=64, name="grouped%d" % i)
-            source = raws[i][:].rearrange("p j t -> p t j")
-            if v < n:
-                nc.scalar.copy(grouped[:, v:n, :], source[:, v:n, :])
-            if v > 0:
-                nc.vector.tensor_copy(grouped[:, 0:v, :], source[:, 0:v, :])
-            return grouped
+        grouped = [keep.tile([P, T, PACK], BF16, align_bytes=64, name="grouped%d" % a) for a in range(2)]
 
-        def quantise(i, grouped):
-            a, t0, n, v = CHUNKS[i]
+        def cast_pair(u):
+            source = pairs[u][:].rearrange("p j t -> p t j")
+            target = grouped[0][:, :, 2 * u : 2 * u + 2]
+            v = PAIR_VECTOR
+            nc.vector.tensor_copy(target[:, 0:v, :], source[:, 0:v, :])
+            nc.scalar.copy(target[:, v:T, :], source[:, v:T, :])
+
+        def cast(i):
+            t0, n, v = CHUNKS[i]
+            source = raws[i][:].rearrange("p j t -> p t j")
+            nc.scalar.copy(grouped[1][:, t0 + v : t0 + n, :], source[:, v:n, :])
+            if v > 0:
+                nc.vector.tensor_copy(grouped[1][:, t0 : t0 + v, :], source[:, 0:v, :])
+
+        def quantise(a, t0, n):
             nc.vector.quantize_mx(
                 out=words[a][:, t0 : t0 + n].bitcast(E4M3X4),
                 scales=token_bytes[SCALE_ROW[a] : P, t0 : t0 + n],
-                in_=grouped[:].rearrange("p t j -> p (t j)"),
+                in_=grouped[a][:, t0 : t0 + n, :].rearrange("p t j -> p (t j)"),
             )
 
         def gather(dst, src, s0, n):
             nc.vector.tensor_copy(dst[:, s0 : s0 + n], src[:].indirect(offs_sb[:, s0 // 16 : (s0 + n) // 16]))
 
-        g = [cast(0), cast(1)]
-        quantise(0, g[0])
-        g.append(cast(2))
-        quantise(1, g[1])
-        quantise(2, g[2])
-        g.append(cast(3))
+        cast_pair(0)
+        cast_pair(1)
+        quantise(0, 0, 512)
+        quantise(0, 512, 256)
+        cast(0)
         gather(slot_words[0], words[0], 0, 512)
+        cast(1)
         gather(slot_words[0], words[0], 512, 512)
-        g.append(cast(4))
-        quantise(3, g[3])
-        g.append(cast(5))
-        quantise(4, g[4])
-        quantise(5, g[5])
+        quantise(1, 0, 256)
+        cast(2)
+        quantise(1, 256, 256)
+        quantise(1, 512, 256)
 
-        banks = {}
+        banks = [psum.tile([P, 128], F32, name="bank%d" % i) for i in range(SLOTS // 128)]
 
-        def multiply(s0):
+        def multiply(a, i):
+            s0 = 128 * i
             e = s0 // C
-            bank = psum.tile([P, 128], F32, name="bank%d" % (s0 // 128))
             nc.tensor.matmul_mx(
-                out=bank[:],
-                lhsT=w8[:, e, :].bitcast(E4M3X4),
-                lhsT_scale=s8[:, e * N : (e + 1) * N],
-                rhs=slot_words[0][:, s0 : s0 + 128].bitcast(E4M3X4),
-                rhs_scale=slot_bytes[SCALE_ROW[0] : P, s0 : s0 + 128],
-                start=True,
-                stop=False,
+                out=banks[i][:],
+                lhsT=(w8[:, e, :].bitcast(E4M3X4), w4[:, e, :].bitcast(E2M1X4))[a],
+                lhsT_scale=(s8, s4)[a][:, e * N : (e + 1) * N],
+                rhs=slot_words[a][:, s0 : s0 + 128].bitcast(E4M3X4),
+                rhs_scale=slot_bytes[SCALE_ROW[a] : P, s0 : s0 + 128],
+                start=(a == 0),
+                stop=(a == 1),
             )
-            nc.tensor.matmul_mx(
-                out=bank[:],
-                lhsT=w4[:, e, :].bitcast(E2M1X4),
-                lhsT_scale=s4[:, e * N : (e + 1) * N],
-                rhs=slot_words[1][:, s0 : s0 + 128].bitcast(E4M3X4),
-                rhs_scale=slot_bytes[SCALE_ROW[1] : P, s0 : s0 + 128],
-                start=False,
-                stop=True,
-            )
-            nc.scalar.activation(y[:, s0 : s0 + 128], bank[:], IDENTITY, bias=bias[:, e : e + 1], scale=1.0)
+
+        for s0 in (0, 512):
+            gather(slot_bytes, token_bytes, s0, 512)
+            for i in range(s0 // 128, s0 // 128 + 4):
+                multiply(0, i)
 
         for s0, n in ((0, 512), (512, 384), (896, 128)):
-            gather(slot_bytes, token_bytes, s0, n)
             gather(slot_words[1], words[1], s0, n)
-            for s in range(s0, s0 + n, 128):
-                multiply(s)
+            for i in range(s0 // 128, (s0 + n) // 128):
+                multiply(1, i)
+                e = i // 2
+                cols = slice(128 * i, 128 * i + 128)
+                if i < 7:
+                    nc.scalar.activation(y[:, cols], banks[i][:], IDENTITY, bias=bias[:, e : e + 1], scale=1.0)
+                else:
+                    nc.vector.tensor_scalar(y[:, cols], banks[i][:], bias[:, e : e + 1], None, ADD)
 
         first = keep.tile([P, T], F32, align_bytes=64, name="first")
         second = keep.tile([P, T], F32, align_bytes=64, name="second")
         result = keep.tile([P, T], F32, align_bytes=64, name="result")
-        PARTS = ((0, 512), (512, 256))
-        for t0, n in PARTS:
+
+        def weigh(target, which, entries_sb, t0, n):
             cols = slice(t0, t0 + n)
-            entries = slice(t0 // 16, (t0 + n) // 16)
-            nc.vector.tensor_tensor(first[:, cols], y[:].indirect(pos1_sb[:, entries]), gates[:, 0, cols], MULT)
-            nc.vector.tensor_tensor(second[:, cols], y[:].indirect(pos2_sb[:, entries]), gates[:, 1, cols], MULT)
+            nc.vector.tensor_tensor(target[:, cols], y[:].indirect(entries_sb[:, t0 // 16 : (t0 + n) // 16]), gates[:, which, cols], MULT)
+
+        def finish(t0, n):
+            cols = slice(t0, t0 + n)
             nc.vector.tensor_tensor(result[:, cols], first[:, cols], second[:, cols], ADD)
             nc.sync.dma_start(out=out[:, cols], in_=result[:, cols])
+
+        weigh(first, 0, pos1_sb, 0, T)
+        weigh(second, 1, pos2_sb, 0, 512)
+        weigh(second, 1, pos2_sb, 512, 256)
+        finish(0, 512)
+        finish(512, 256)

@@ -22,8 +22,13 @@ MULT = mybir.AluOpType.mult
 ADD = mybir.AluOpType.add
 IDENTITY = mybir.ActivationFunctionType.Identity
 
-PAIR_VECTOR = 512
-CHUNKS = ((0, 256, 0), (256, 256, 0), (512, 256, 160))
+CHUNKS = (
+    (0, 0, 512, 320),
+    (0, 512, 256, 160),
+    (1, 0, 256, 0),
+    (1, 256, 256, 0),
+    (1, 512, 256, 160),
+)
 SCALE_ROW = (4, 0)
 
 
@@ -45,7 +50,7 @@ def tile_moe_cap2_lin_bias_kernel(
         nc.vector.memset(s8[:].bitcast(I32), 0)
         nc.vector.memset(s4[:].bitcast(I32), 0)
         token_bytes = keep.tile([P, T], U8, align_bytes=64, name="token_bytes")
-        nc.gpsimd.memset(token_bytes[:], 0)
+        nc.vector.memset(token_bytes[:].bitcast(I32), 0)
         y = keep.tile([P, SLOTS + PAD], F32, align_bytes=64, name="y")
         nc.vector.memset(y[:, SLOTS:], 0.0)
 
@@ -57,18 +62,14 @@ def tile_moe_cap2_lin_bias_kernel(
                     in_=scales[:, 0, 4 * q : 4 * q + 4, :].rearrange("e q n -> q e n").bitcast(I32),
                 )
 
-        pairs = []
-        by_row = xT[0:512, :].rearrange("(p j) t -> p j t", j=PACK)
-        for u in range(2):
-            pair = keep.tile([P, 2, T], F32, align_bytes=64, name="pair%d" % u)
-            nc.sync.dma_start(out=pair[:], in_=by_row[:, 2 * u : 2 * u + 2, :])
-            pairs.append(pair)
-        nc.sync.dma_start(offs_sb[:], offs)
         raws = []
-        for i, (t0, n, v) in enumerate(CHUNKS):
+        for i, (a, t0, n, v) in enumerate(CHUNKS):
             raw = keep.tile([P, PACK, n], F32, align_bytes=64, name="raw%d" % i)
-            nc.sync.dma_start(out=raw[:], in_=xT[512:1024, t0 : t0 + n].rearrange("(p j) t -> p j t", j=PACK))
+            rows = xT[a * 512 : (a + 1) * 512, t0 : t0 + n]
+            nc.sync.dma_start(out=raw[:], in_=rows.rearrange("(p j) t -> p j t", j=PACK))
             raws.append(raw)
+            if i == 1:
+                nc.sync.dma_start(offs_sb[:], offs)
 
         w8 = keep.tile([P, E, 4 * N], U8, align_bytes=64, name="w8")
         nc.sync.dma_start(out=w8[:].bitcast(I32), in_=w8_words[:, 0].rearrange("e p n r -> p e (n r)").bitcast(I32))
@@ -87,19 +88,12 @@ def tile_moe_cap2_lin_bias_kernel(
 
         grouped = [keep.tile([P, T, PACK], BF16, align_bytes=64, name="grouped%d" % a) for a in range(2)]
 
-        def cast_pair(u):
-            source = pairs[u][:].rearrange("p j t -> p t j")
-            target = grouped[0][:, :, 2 * u : 2 * u + 2]
-            v = PAIR_VECTOR
-            nc.vector.tensor_copy(target[:, 0:v, :], source[:, 0:v, :])
-            nc.scalar.copy(target[:, v:T, :], source[:, v:T, :])
-
         def cast(i):
-            t0, n, v = CHUNKS[i]
+            a, t0, n, v = CHUNKS[i]
             source = raws[i][:].rearrange("p j t -> p t j")
-            nc.scalar.copy(grouped[1][:, t0 + v : t0 + n, :], source[:, v:n, :])
             if v > 0:
-                nc.vector.tensor_copy(grouped[1][:, t0 : t0 + v, :], source[:, 0:v, :])
+                nc.vector.tensor_copy(grouped[a][:, t0 : t0 + v, :], source[:, 0:v, :])
+            nc.scalar.copy(grouped[a][:, t0 + v : t0 + n, :], source[:, v:n, :])
 
         def quantise(a, t0, n):
             nc.vector.quantize_mx(
@@ -111,18 +105,19 @@ def tile_moe_cap2_lin_bias_kernel(
         def gather(dst, src, s0, n):
             nc.vector.tensor_copy(dst[:, s0 : s0 + n], src[:].indirect(offs_sb[:, s0 // 16 : (s0 + n) // 16]))
 
-        cast_pair(0)
-        cast_pair(1)
-        quantise(0, 0, 512)
-        quantise(0, 512, 256)
         cast(0)
-        gather(slot_words[0], words[0], 0, 512)
+        quantise(0, 0, 512)
         cast(1)
-        gather(slot_words[0], words[0], 512, 512)
-        quantise(1, 0, 256)
+        quantise(0, 512, 256)
+        gather(slot_words[0], words[0], 0, 512)
         cast(2)
+        gather(slot_words[0], words[0], 512, 384)
+        cast(3)
+        quantise(1, 0, 256)
+        cast(4)
         quantise(1, 256, 256)
         quantise(1, 512, 256)
+        gather(slot_words[0], words[0], 896, 128)
 
         banks = [psum.tile([P, 128], F32, name="bank%d" % i) for i in range(SLOTS // 128)]
 
@@ -150,7 +145,7 @@ def tile_moe_cap2_lin_bias_kernel(
                 multiply(1, i)
                 e = i // 2
                 cols = slice(128 * i, 128 * i + 128)
-                if i < 7:
+                if i != 6:
                     nc.scalar.activation(y[:, cols], banks[i][:], IDENTITY, bias=bias[:, e : e + 1], scale=1.0)
                 else:
                     nc.vector.tensor_scalar(y[:, cols], banks[i][:], bias[:, e : e + 1], None, ADD)
@@ -168,8 +163,10 @@ def tile_moe_cap2_lin_bias_kernel(
             nc.vector.tensor_tensor(result[:, cols], first[:, cols], second[:, cols], ADD)
             nc.sync.dma_start(out=out[:, cols], in_=result[:, cols])
 
-        weigh(first, 0, pos1_sb, 0, T)
+        weigh(first, 0, pos1_sb, 0, 512)
         weigh(second, 1, pos2_sb, 0, 512)
+        weigh(first, 0, pos1_sb, 512, 256)
+        finish(0, 256)
         weigh(second, 1, pos2_sb, 512, 256)
-        finish(0, 512)
+        finish(256, 256)
         finish(512, 256)

@@ -23,11 +23,11 @@ ADD = mybir.AluOpType.add
 IDENTITY = mybir.ActivationFunctionType.Identity
 
 CHUNKS = (
-    (0, 0, 512, 320),
-    (0, 512, 256, 160),
+    (0, 0, 512, 352),
+    (0, 512, 256, 176),
     (1, 0, 256, 0),
     (1, 256, 256, 0),
-    (1, 512, 256, 160),
+    (1, 512, 256, 96),
 )
 SCALE_ROW = (4, 0)
 
@@ -54,7 +54,7 @@ def tile_moe_cap2_lin_bias_kernel(
         y = keep.tile([P, SLOTS + PAD], F32, align_bytes=64, name="y")
         nc.vector.memset(y[:, SLOTS:], 0.0)
 
-        for plane, scales, queue in ((s4, w4_scales, nc.scalar), (s8, w8_scales, nc.gpsimd)):
+        for plane, scales, queue in ((s8, w8_scales, nc.gpsimd), (s4, w4_scales, nc.gpsimd)):
             view = plane[:].rearrange("p (e n) -> p e n", e=E)
             for q in range(4):
                 queue.dma_start(
@@ -90,10 +90,12 @@ def tile_moe_cap2_lin_bias_kernel(
 
         def cast(i):
             a, t0, n, v = CHUNKS[i]
-            source = raws[i][:].rearrange("p j t -> p t j")
-            if v > 0:
-                nc.vector.tensor_copy(grouped[a][:, t0 : t0 + v, :], source[:, 0:v, :])
-            nc.scalar.copy(grouped[a][:, t0 + v : t0 + n, :], source[:, v:n, :])
+            for copy, c0, c1 in ((nc.vector.tensor_copy, 0, v), (nc.scalar.copy, v, n)):
+                if c0 < c1:
+                    copy(
+                        grouped[a][:, t0 + c0 : t0 + c1, :].rearrange("p (c i) j -> p c j i", i=4),
+                        raws[i][:, :, c0:c1].rearrange("p j (c i) -> p c j i", i=4),
+                    )
 
         def quantise(a, t0, n):
             nc.vector.quantize_mx(

from contextlib import ExitStack

import concourse.mybir as mybir

K, T, E, C, N = 1024, 768, 4, 256, 128
PAD = 32
P = 128
PACK = 4
SLOTS = E * C
FLOPS = 2 * K * N * SLOTS

F32 = mybir.dt.float32
BF16 = mybir.dt.bfloat16
I32 = mybir.dt.int32
U32 = mybir.dt.uint32
U16 = mybir.dt.uint16
U8 = mybir.dt.uint8
E4M3X4 = mybir.dt.float8_e4m3fn_x4
E2M1X4 = mybir.dt.float4_e2m1fn_x4

MULT = mybir.AluOpType.mult
ADD = mybir.AluOpType.add
IDENTITY = mybir.ActivationFunctionType.Identity

CHUNKS = (
    (0, 0, 512, 352),
    (0, 512, 256, 176),
    (1, 0, 256, 0),
    (1, 256, 256, 0),
    (1, 512, 256, 96),
)
SCALE_ROW = (4, 0)


def tile_moe_cap2_lin_bias_kernel(
    tc, xT, w8_words, w8_scales, w4_words, w4_scales, b, gate, offs, pos1, pos2, out
):
    nc = tc.nc
    with ExitStack() as ctx:
        lists = ctx.enter_context(tc.tile_pool(name="lists", bufs=1))
        keep = ctx.enter_context(tc.tile_pool(name="keep", bufs=1))
        psum = ctx.enter_context(tc.psum_pool(name="psum", bufs=1))

        offs_sb = lists.tile([P, SLOTS // 16], U16, name="offs_sb")
        pos1_sb = lists.tile([P, T // 16], U16, name="pos1_sb")
        pos2_sb = lists.tile([P, T // 16], U16, name="pos2_sb")

        s8 = keep.tile([P, E * N], U8, align_bytes=64, name="s8")
        s4 = keep.tile([P, E * N], U8, align_bytes=64, name="s4")
        nc.vector.memset(s8[:].bitcast(I32), 0)
        nc.vector.memset(s4[:].bitcast(I32), 0)
        token_bytes = keep.tile([P, T], U8, align_bytes=64, name="token_bytes")
        nc.vector.memset(token_bytes[:].bitcast(I32), 0)
        y = keep.tile([P, SLOTS + PAD], F32, align_bytes=64, name="y")
        nc.vector.memset(y[:, SLOTS:], 0.0)

        for plane, scales, queue in ((s8, w8_scales, nc.gpsimd), (s4, w4_scales, nc.gpsimd)):
            view = plane[:].rearrange("p (e n) -> p e n", e=E)
            for q in range(4):
                queue.dma_start(
                    out=view[32 * q : 32 * q + 4, :, :].bitcast(I32),
                    in_=scales[:, 0, 4 * q : 4 * q + 4, :].rearrange("e q n -> q e n").bitcast(I32),
                )

        raws = []
        for i, (a, t0, n, v) in enumerate(CHUNKS):
            raw = keep.tile([P, PACK, n], F32, align_bytes=64, name="raw%d" % i)
            rows = xT[a * 512 : (a + 1) * 512, t0 : t0 + n]
            nc.sync.dma_start(out=raw[:], in_=rows.rearrange("(p j) t -> p j t", j=PACK))
            raws.append(raw)
            if i == 1:
                nc.sync.dma_start(offs_sb[:], offs)

        w8 = keep.tile([P, E, 4 * N], U8, align_bytes=64, name="w8")
        nc.sync.dma_start(out=w8[:].bitcast(I32), in_=w8_words[:, 0].rearrange("e p n r -> p e (n r)").bitcast(I32))
        w4 = keep.tile([P, E, 2 * N], U8, align_bytes=64, name="w4")
        nc.sync.dma_start(out=w4[:].bitcast(I32), in_=w4_words[:, 0].rearrange("e p n -> p e n").bitcast(I32))
        bias = keep.tile([P, E], F32, name="bias")
        nc.sync.dma_start(out=bias[:], in_=b)
        nc.sync.dma_start(pos1_sb[:], pos1)
        nc.sync.dma_start(pos2_sb[:], pos2)
        gates = keep.tile([P, 2, T], F32, align_bytes=64, name="gates")
        nc.sync.dma_start(out=gates[:], in_=gate.rearrange("a p t -> p a t"))

        words = [keep.tile([P, T], U32, align_bytes=64, name="words%d" % a) for a in range(2)]
        slot_words = [keep.tile([P, SLOTS], U32, align_bytes=64, name="slot_words%d" % a) for a in range(2)]
        slot_bytes = keep.tile([P, SLOTS], U8, align_bytes=64, name="slot_bytes")

        grouped = [keep.tile([P, T, PACK], BF16, align_bytes=64, name="grouped%d" % a) for a in range(2)]

        def cast(i):
            a, t0, n, v = CHUNKS[i]
            for copy, c0, c1 in ((nc.vector.tensor_copy, 0, v), (nc.scalar.copy, v, n)):
                if c0 < c1:
                    copy(
                        grouped[a][:, t0 + c0 : t0 + c1, :].rearrange("p (c i) j -> p c j i", i=4),
                        raws[i][:, :, c0:c1].rearrange("p j (c i) -> p c j i", i=4),
                    )

        def quantise(a, t0, n):
            nc.vector.quantize_mx(
                out=words[a][:, t0 : t0 + n].bitcast(E4M3X4),
                scales=token_bytes[SCALE_ROW[a] : P, t0 : t0 + n],
                in_=grouped[a][:, t0 : t0 + n, :].rearrange("p t j -> p (t j)"),
            )

        def gather(dst, src, s0, n):
            nc.vector.tensor_copy(dst[:, s0 : s0 + n], src[:].indirect(offs_sb[:, s0 // 16 : (s0 + n) // 16]))

        cast(0)
        quantise(0, 0, 512)
        cast(1)
        quantise(0, 512, 256)
        gather(slot_words[0], words[0], 0, 512)
        cast(2)
        gather(slot_words[0], words[0], 512, 384)
        cast(3)
        quantise(1, 0, 256)
        cast(4)
        quantise(1, 256, 256)
        quantise(1, 512, 256)
        gather(slot_words[0], words[0], 896, 128)

        banks = [psum.tile([P, 128], F32, name="bank%d" % i) for i in range(SLOTS // 128)]

        def multiply(a, i):
            s0 = 128 * i
            e = s0 // C
            nc.tensor.matmul_mx(
                out=banks[i][:],
                lhsT=(w8[:, e, :].bitcast(E4M3X4), w4[:, e, :].bitcast(E2M1X4))[a],
                lhsT_scale=(s8, s4)[a][:, e * N : (e + 1) * N],
                rhs=slot_words[a][:, s0 : s0 + 128].bitcast(E4M3X4),
                rhs_scale=slot_bytes[SCALE_ROW[a] : P, s0 : s0 + 128],
                start=(a == 0),
                stop=(a == 1),
            )

        for s0 in (0, 512):
            gather(slot_bytes, token_bytes, s0, 512)
            for i in range(s0 // 128, s0 // 128 + 4):
                multiply(0, i)

        for s0, n in ((0, 512), (512, 384), (896, 128)):
            gather(slot_words[1], words[1], s0, n)
            for i in range(s0 // 128, (s0 + n) // 128):
                multiply(1, i)
                e = i // 2
                cols = slice(128 * i, 128 * i + 128)
                if i != 6:
                    nc.scalar.activation(y[:, cols], banks[i][:], IDENTITY, bias=bias[:, e : e + 1], scale=1.0)
                else:
                    nc.vector.tensor_scalar(y[:, cols], banks[i][:], bias[:, e : e + 1], None, ADD)

        first = keep.tile([P, T], F32, align_bytes=64, name="first")
        second = keep.tile([P, T], F32, align_bytes=64, name="second")
        result = keep.tile([P, T], F32, align_bytes=64, name="result")

        def weigh(target, which, entries_sb, t0, n):
            cols = slice(t0, t0 + n)
            nc.vector.tensor_tensor(target[:, cols], y[:].indirect(entries_sb[:, t0 // 16 : (t0 + n) // 16]), gates[:, which, cols], MULT)

        def finish(t0, n):
            cols = slice(t0, t0 + n)
            nc.vector.tensor_tensor(result[:, cols], first[:, cols], second[:, cols], ADD)
            nc.sync.dma_start(out=out[:, cols], in_=result[:, cols])

        weigh(first, 0, pos1_sb, 0, 512)
        weigh(second, 1, pos2_sb, 0, 512)
        weigh(first, 0, pos1_sb, 512, 256)
        finish(0, 256)
        weigh(second, 1, pos2_sb, 512, 256)
        finish(256, 256)
        finish(512, 256)
